import numpy as np
import ml_dtypes


def mxq(x, axis, fmt="e4m3"):
    dtype, down = {"e4m3": (ml_dtypes.float8_e4m3fn, 7), "e5m2": (ml_dtypes.float8_e5m2, 14)}[fmt]
    v = np.moveaxis(np.asarray(x, np.float32).astype(ml_dtypes.bfloat16).astype(np.float64), axis, -1)
    blocks = v.reshape(v.shape[:-1] + (-1, 32))
    amax = np.abs(blocks).max(-1, keepdims=True)
    byte = np.maximum(np.where(amax > 0, np.frexp(amax)[1] - 1 + 127, 0) - down, 1)
    scale = np.exp2(byte - 127.0)
    codes = (blocks / scale).astype(np.float32).astype(dtype).astype(np.float64)
    return np.moveaxis((codes * scale).reshape(v.shape), -1, axis)


WIDE = False


def mx_kscale(k):
    if not WIDE:
        return np.ones(k)
    levels = np.array([30, -30])
    if k % 512:
        return np.exp2(np.random.permutation(np.resize(levels, k // 32))).repeat(32)
    a = np.empty((k // 512, 16))
    for p in range(k // 512):
        a[p, :8] = np.random.permutation(np.resize(levels, 8))
        for g in range(8):
            far = levels[np.abs(levels - a[p, g]) >= 10]
            a[p, g + 8] = far[np.random.randint(len(far))]
    return np.exp2(a.ravel()).repeat(32)


def f64(x):
    return np.asarray(x).astype(np.float64)


def striped(idx):
    return np.tile(np.asarray(idx).reshape(-1, 16).T, (8, 1)).astype(np.uint16)


def unstriped(offs):
    return offs[:16].T.reshape(-1).astype(np.int64)


E2M1 = np.array([0.0, 0.5, 1.0, 1.5, 2.0, 3.0, 4.0, 6.0, -0.0, -0.5, -1.0, -1.5, -2.0, -3.0, -4.0, -6.0])


def pack_weight(w, fmt):
    k, n = w.shape
    w = f64(np.asarray(w, np.float32).astype(ml_dtypes.bfloat16)).reshape(k // 32, 32, n)
    amax = np.abs(w).max(1)
    if fmt == "e4m3":
        byte = np.frexp(amax)[1] - 1 + 127 - 7
    else:
        mant, ex = np.frexp(amax / 6.0)
        byte = np.where(mant > 0.5, ex, ex - 1) + 127
    byte = np.clip(np.where(amax > 0, byte, 1), 1, 254)
    scaled = (w * np.exp2(127.0 - byte)[:, None, :]).reshape(k, n).astype(np.float32)
    by_word = np.ascontiguousarray(scaled.reshape(k // 512, 128, 4, n).transpose(0, 1, 3, 2))
    if fmt == "e4m3":
        words = by_word.astype(ml_dtypes.float8_e4m3fn).view(np.uint8)
    else:
        c = by_word.astype(ml_dtypes.float4_e2m1fn).view(np.uint8) & 0xF
        words = (c[..., 0::2] | (c[..., 1::2] << 4)).reshape(k // 512, 128, 2 * n)
    return np.ascontiguousarray(words), np.ascontiguousarray(byte.astype(np.uint8).reshape(k // 512, 16, n))


def unpack_weight(words, scales, fmt):
    g, _, n = scales.shape
    words = np.ascontiguousarray(words).reshape(g, 128, n, -1)
    if fmt == "e4m3":
        vals = words.view(ml_dtypes.float8_e4m3fn).astype(np.float64)
    else:
        nib = np.empty((g, 128, n, 4), np.uint8)
        nib[..., 0::2] = words & 0xF
        nib[..., 1::2] = words >> 4
        vals = E2M1[nib]
    vals = vals * np.repeat(np.exp2(scales.astype(np.float64) - 127.0), 8, axis=1)[..., None]
    return vals.transpose(0, 1, 3, 2).reshape(g * 512, n)


def bf(x):
    return np.asarray(x, np.float32).astype(ml_dtypes.bfloat16)


def planes(Y):
    r, m = Y.shape
    b = f64(bf(Y)).reshape(r // 32, 32, m)
    amax = np.abs(b).max(1)
    byte = np.clip(np.where(amax > 0, np.frexp(amax)[1] - 1 + 127 - 7, 1), 1, 254)
    codes = (b * np.exp2(127.0 - byte)[:, None, :]).reshape(r, m).astype(np.float32).astype(ml_dtypes.float8_e4m3fn).view(np.uint8)
    words = codes.reshape(r // 512, 128, 4, m).transpose(0, 1, 3, 2)
    return np.ascontiguousarray(words), np.ascontiguousarray(byte.astype(np.uint8).reshape(r // 512, 16, m))


T, K, V, N, J = 1024, 512, 1024, 512, 128


def setup_inputs():
    n = np.random.standard_normal
    idx = np.random.permutation(V)[:J]
    ft = mx_kscale(T)
    fn = mx_kscale(N)
    gp = pack_weight(n((N, J)) / fn[:, None], "e2m1")
    wp = pack_weight(n((N, K)) * 1 / np.sqrt(N) * fn[:, None], "e4m3")
    return {
        "h2": (n((T, K)) * ft[:, None]).astype(np.float32),
        "e": (n((T, V)) / ft[:, None]).astype(np.float32),
        "g_words": gp[0],
        "g_scales": gp[1],
        "w_words": wp[0],
        "w_scales": wp[1],
        "offs": striped(idx),
    }


def reference(h2, e, g_words, g_scales, w_words, w_scales, offs):
    idx = unstriped(offs)
    gu = unpack_weight(g_words, g_scales, "e2m1")
    wu = unpack_weight(w_words, w_scales, "e4m3")
    h2q = mxq(f64(h2), 0, "e4m3")
    eq = mxq(f64(e), 0, "e5m2")
    o = h2q.T @ eq
    dx = wu.T @ gu
    p = np.zeros((K, V))
    p[:, idx] = dx
    y = 0.03 * o + p
    words, scales = planes(y)
    return y, words, scales

@@ -1,0 +1,180 @@
+from contextlib import ExitStack
+
+import concourse.mybir as mybir
+
+T, K, V, N, J = 1024, 512, 1024, 512, 128
+FLOPS = 2 * T * K * V + 2 * N * K * J
+
+F32 = mybir.dt.float32
+BF16 = mybir.dt.bfloat16
+I32 = mybir.dt.int32
+U32 = mybir.dt.uint32
+U16 = mybir.dt.uint16
+U8 = mybir.dt.uint8
+E4M3 = mybir.dt.float8_e4m3fn_x4
+E5M2 = mybir.dt.float8_e5m2_x4
+E2M1 = mybir.dt.float4_e2m1fn_x4
+MULT = mybir.AluOpType.mult
+ADD = mybir.AluOpType.add
+
+P = 128
+PACK = 4
+PASS = P * PACK
+HALF = 512
+ALPHA = 0.03
+
+FIRST_VEC = (128, 128)
+H_VEC = (0, 0)
+E_VEC = {(0, 0): 0, (1, 0): 64, (0, 1): 0}
+LAST_VEC = (64, 160)
+Y_VEC = (128, 320)
+
+
+def tile_list_tied_table_grad_pl_kernel(tc, h2, e, g_words, g_scales, w_words, w_scales, offs, out_0, out_1, out_2):
+    nc = tc.nc
+    with ExitStack() as ctx:
+        sb = ctx.enter_context(tc.tile_pool(name="sb", bufs=1))
+        ps = ctx.enter_context(tc.psum_pool(name="ps", bufs=1))
+
+        offsets = sb.tile([P, J // 16], U16, name="offsets")
+        w_raw = sb.tile([P, K], I32, name="w_raw", align_bytes=64)
+        g_codes = sb.tile([P, 2 * J], U8, name="g_codes", align_bytes=64)
+        ws_raw = sb.tile([P, K], U8, name="ws_raw", align_bytes=64)
+        g_plane = sb.tile([P, J], U8, name="g_plane", align_bytes=64)
+
+        def load_plane(eng, tile, scales, q):
+            rows = scales[0, 4 * q:4 * q + 4, :].bitcast(I32)
+            eng.dma_start(out=tile[32 * q:32 * q + 32, :].bitcast(I32), in_=rows.unsqueeze(0).broadcast_to([8, 4, rows.shape[1]]))
+
+        def load_rows(name, src, a, c0, width):
+            raw = sb.tile([P, PACK, width], F32, name=name)
+            nc.sync.dma_start(out=raw[:], in_=src[a * PASS:(a + 1) * PASS, c0:c0 + width].rearrange("(p j) c -> p j c", j=PACK))
+            return raw
+
+        for q in range(4):
+            load_plane(nc.scalar, ws_raw, w_scales, q)
+        nc.sync.dma_start(out=w_raw[:], in_=w_words[0].rearrange("p c r -> p (c r)").bitcast(I32))
+        nc.sync.dma_start(out=g_codes[:].bitcast(I32), in_=g_words[0].bitcast(I32))
+        load_plane(nc.sync, g_plane, g_scales, 0)
+        first_raw = [load_rows("e_first0", e, 0, 0, 256)]
+        for q in range(1, 4):
+            load_plane(nc.sync, g_plane, g_scales, q)
+        first_raw.append(load_rows("e_first1", e, 0, 256, 256))
+        nc.sync.dma_start(offsets[:], offs)
+        h_raw = [load_rows("h_raw%d" % a, h2, a, 0, K) for a in range(2)]
+        e_raw = {}
+        e_raw[(1, 0)] = load_rows("e_raw10", e, 1, 0, HALF)
+        e_raw[(0, 1)] = load_rows("e_raw01", e, 0, HALF, HALF)
+        last_raw = [load_rows("e_last%d" % u, e, 1, HALF + 256 * u, 256) for u in range(2)]
+
+        pages = [sb.tile([P, V], F32, name="page%d" % r) for r in range(PACK)]
+        for r in range(PACK):
+            nc.vector.memset(pages[r][:], 0.0)
+
+        w_codes = sb.tile([P, PACK, P], I32, name="w_codes", align_bytes=64)
+        w_plane = sb.tile([P, PACK, P], U8, name="w_plane", align_bytes=64)
+        nc.vector.tensor_copy(out=w_codes[:].rearrange("p r m -> p m r"), in_=w_raw[:].rearrange("p (m r) -> p m r", r=PACK))
+        nc.vector.tensor_copy(out=w_plane[:], in_=ws_raw[:].rearrange("p (m r) -> p r m", r=PACK))
+        dx_ps = ps.tile([P, PACK, J], F32, name="dx_ps", tag="bank7")
+        for r in range(PACK):
+            nc.tensor.matmul_mx(out=dx_ps[:, r, :], lhsT=w_codes[:, r, :].bitcast(E4M3), lhsT_scale=w_plane[:, r, :],
+                                rhs=g_codes[:].bitcast(E2M1), rhs_scale=g_plane[:], start=True, stop=True)
+        dx = sb.tile([P, PACK, J], F32, name="dx")
+        nc.scalar.copy(out=dx[:], in_=dx_ps[:])
+
+        def weave(dst, src, width, vec_cols):
+            for eng, lo, hi in ((0, 0, vec_cols), (1, vec_cols, width)):
+                if hi > lo:
+                    o = dst[:, lo:hi, :].rearrange("p (c i) j -> p c j i", i=4)
+                    s = src[:, :, lo:hi].rearrange("p j (c i) -> p c j i", i=4)
+                    if eng == 0:
+                        nc.vector.tensor_copy(out=o, in_=s)
+                    else:
+                        nc.scalar.copy(out=o, in_=s)
+
+        def weave_h(a):
+            hb = sb.tile([P, PACK, P, PACK], BF16, name="hb%d" % a, align_bytes=64)
+            o = hb[:].rearrange("p r m j -> p m j r")
+            s = h_raw[a][:].rearrange("p j (m r) -> p m j r", r=PACK)
+            v = H_VEC[a]
+            if v > 0:
+                nc.vector.tensor_copy(out=o[:, 0:v], in_=s[:, 0:v])
+            if v < P:
+                nc.scalar.copy(out=o[:, v:P], in_=s[:, v:P])
+            return hb
+
+        def quant_h(a, hb):
+            codes = sb.tile([P, K], U32, name="h_codes%d" % a, align_bytes=64)
+            plane = sb.tile([P, K], U8, name="h_plane%d" % a, align_bytes=64)
+            nc.vector.quantize_mx(out=codes[:].bitcast(E4M3), scales=plane[:], in_=hb[:].rearrange("p r m j -> p (r m j)"))
+            return codes, plane
+
+        def e_tiles(a, half):
+            codes = sb.tile([P, HALF], U32, name="e_codes%d%d" % (a, half), align_bytes=64)
+            plane = sb.tile([P, HALF], U8, name="e_plane%d%d" % (a, half), align_bytes=64)
+            return codes, plane
+
+        def weave_e(name, raw, width, vec_cols):
+            eb = sb.tile([P, width, PACK], BF16, name=name, align_bytes=64)
+            weave(eb, raw, width, vec_cols)
+            return eb
+
+        def quant_e(eb, tiles, c0, width):
+            nc.vector.quantize_mx(out=tiles[0][:, c0:c0 + width].bitcast(E5M2), scales=tiles[1][:, c0:c0 + width],
+                                  in_=eb[:].rearrange("p c j -> p (c j)"))
+
+        def passes(acc, a, hq, eq):
+            for r in range(PACK):
+                cols = slice(r * P, (r + 1) * P)
+                nc.tensor.matmul_mx(out=acc[r][:], lhsT=hq[0][:, cols].bitcast(E4M3), lhsT_scale=hq[1][:, cols],
+                                    rhs=eq[0][:].bitcast(E5M2), rhs_scale=eq[1][:], start=(a == 0), stop=(a == 1))
+
+        y_rows = out_0.rearrange("(p r) v -> p r v", r=PACK)
+        y_words = out_1[0].rearrange("p c r -> p (c r)").bitcast(I32)
+        y_plane = sb.tile([P, V], U8, name="y_plane", align_bytes=64)
+
+        def finish(half, acc):
+            cols = slice(half * HALF, (half + 1) * HALF)
+            y = sb.tile([P, PACK, HALF], F32, name="y%d" % half)
+            for r in range(PACK):
+                nc.vector.scalar_tensor_tensor(out=y[:, r, :], in0=acc[r][:], scalar=ALPHA, in1=pages[r][:, cols], op0=MULT, op1=ADD)
+                nc.sync.dma_start(out=y_rows[:, r, cols], in_=y[:, r, :])
+            yb = sb.tile([P, HALF, PACK], BF16, name="yb%d" % half, align_bytes=64)
+            weave(yb, y, HALF, Y_VEC[half])
+            codes = sb.tile([P, HALF], U32, name="y_codes%d" % half, align_bytes=64)
+            nc.vector.quantize_mx(out=codes[:].bitcast(E4M3), scales=y_plane[:, cols], in_=yb[:].rearrange("p c j -> p (c j)"))
+            nc.sync.dma_start(out=y_words[:, cols], in_=codes[:].bitcast(I32))
+
+        acc0 = [ps.tile([P, HALF], F32, name="acc0_%d" % r, tag="bank%d" % r) for r in range(PACK)]
+
+        eq00 = e_tiles(0, 0)
+        for u in range(2):
+            eb = weave_e("eb00_%d" % u, first_raw[u], 256, FIRST_VEC[u])
+            quant_e(eb, eq00, 256 * u, 256)
+        for r in range(PACK):
+            nc.vector.tensor_copy(pages[r][:].indirect(offsets[:]), dx[:, r, :])
+        hb = weave_h(0)
+        hq0 = quant_h(0, hb)
+        passes(acc0, 0, hq0, eq00)
+        hb = weave_h(1)
+        hq1 = quant_h(1, hb)
+        eb = weave_e("eb10", e_raw[(1, 0)], HALF, E_VEC[(1, 0)])
+        eq10 = e_tiles(1, 0)
+        quant_e(eb, eq10, 0, HALF)
+        passes(acc0, 1, hq1, eq10)
+
+        acc1 = [ps.tile([P, HALF], F32, name="acc1_%d" % r, tag="bank%d" % (4 + r)) for r in range(PACK)]
+        eb = weave_e("eb01", e_raw[(0, 1)], HALF, E_VEC[(0, 1)])
+        finish(0, acc0)
+        eq01 = e_tiles(0, 1)
+        quant_e(eb, eq01, 0, HALF)
+        passes(acc1, 0, hq0, eq01)
+        eq11 = e_tiles(1, 1)
+        for u in range(2):
+            eb = weave_e("eb11_%d" % u, last_raw[u], 256, LAST_VEC[u])
+            quant_e(eb, eq11, 256 * u, 256)
+        passes(acc1, 1, hq1, eq11)
+        finish(1, acc1)
+        for q in range(4):
+            eng = nc.sync if q % 2 == 0 else nc.scalar
+            eng.dma_start(out=out_2[0, 4 * q:4 * q + 4, :].bitcast(I32), in_=y_plane[32 * q:32 * q + 4, :].bitcast(I32))

@@ -22,12 +22,11 @@ PACK = 4
 PASS = P * PACK
 HALF = 512
 ALPHA = 0.03
+LAP = 32
+ORDER = {("h", 0): 0, (0, 0): 1, ("h", 1): 2, (1, 0): 3, (0, 1): 4, (1, 1): 5}
 
-FIRST_VEC = (128, 128)
-H_VEC = (0, 0)
-E_VEC = {(0, 0): 0, (1, 0): 64, (0, 1): 0}
-LAST_VEC = (64, 160)
-Y_VEC = (128, 320)
+H_VEC = 64
+E_VEC = {(0, 0): 0, (1, 0): 320, (0, 1): 0, (1, 1): 512}
 
 
 def tile_list_tied_table_grad_pl_kernel(tc, h2, e, g_words, g_scales, w_words, w_scales, offs, out_0, out_1, out_2):
@@ -47,7 +46,7 @@ def tile_list_tied_table_grad_pl_kernel(tc, h2, e, g_words, g_scales, w_words, w
             eng.dma_start(out=tile[32 * q:32 * q + 32, :].bitcast(I32), in_=rows.unsqueeze(0).broadcast_to([8, 4, rows.shape[1]]))
 
         def load_rows(name, src, a, c0, width):
-            raw = sb.tile([P, PACK, width], F32, name=name)
+            raw = sb.tile([P, PACK, width], F32, name=name, tag=name, align_bytes=64)
             nc.sync.dma_start(out=raw[:], in_=src[a * PASS:(a + 1) * PASS, c0:c0 + width].rearrange("(p j) c -> p j c", j=PACK))
             return raw
 
@@ -56,20 +55,19 @@ def tile_list_tied_table_grad_pl_kernel(tc, h2, e, g_words, g_scales, w_words, w
         nc.sync.dma_start(out=w_raw[:], in_=w_words[0].rearrange("p c r -> p (c r)").bitcast(I32))
         nc.sync.dma_start(out=g_codes[:].bitcast(I32), in_=g_words[0].bitcast(I32))
         load_plane(nc.sync, g_plane, g_scales, 0)
-        first_raw = [load_rows("e_first0", e, 0, 0, 256)]
+        h_first = [load_rows("h_first0", h2, 0, 0, 256)]
         for q in range(1, 4):
             load_plane(nc.sync, g_plane, g_scales, q)
-        first_raw.append(load_rows("e_first1", e, 0, 256, 256))
+        h_first.append(load_rows("h_first1", h2, 0, 256, 256))
         nc.sync.dma_start(offsets[:], offs)
-        h_raw = [load_rows("h_raw%d" % a, h2, a, 0, K) for a in range(2)]
-        e_raw = {}
-        e_raw[(1, 0)] = load_rows("e_raw10", e, 1, 0, HALF)
-        e_raw[(0, 1)] = load_rows("e_raw01", e, 0, HALF, HALF)
-        last_raw = [load_rows("e_last%d" % u, e, 1, HALF + 256 * u, 256) for u in range(2)]
+        e_raw = {(0, 0): load_rows("e_raw00", e, 0, 0, HALF)}
+        h_raw1 = load_rows("h_raw1", h2, 1, 0, K)
+        for a, half in ((1, 0), (0, 1), (1, 1)):
+            e_raw[(a, half)] = load_rows("e_raw%d%d" % (a, half), e, a, half * HALF, HALF)
 
         pages = [sb.tile([P, V], F32, name="page%d" % r) for r in range(PACK)]
         for r in range(PACK):
-            nc.vector.memset(pages[r][:], 0.0)
+            (nc.vector if r < 2 else nc.gpsimd).memset(pages[r][:], 0.0)
 
         w_codes = sb.tile([P, PACK, P], I32, name="w_codes", align_bytes=64)
         w_plane = sb.tile([P, PACK, P], U8, name="w_plane", align_bytes=64)
@@ -80,7 +78,13 @@ def tile_list_tied_table_grad_pl_kernel(tc, h2, e, g_words, g_scales, w_words, w
             nc.tensor.matmul_mx(out=dx_ps[:, r, :], lhsT=w_codes[:, r, :].bitcast(E4M3), lhsT_scale=w_plane[:, r, :],
                                 rhs=g_codes[:].bitcast(E2M1), rhs_scale=g_plane[:], start=True, stop=True)
         dx = sb.tile([P, PACK, J], F32, name="dx")
-        nc.scalar.copy(out=dx[:], in_=dx_ps[:])
+        nc.vector.tensor_copy(out=dx[:], in_=dx_ps[:])
+
+        woven = sb.tile([P, 4 * PASS * PACK], BF16, name="woven", align_bytes=64)
+
+        def slab(n):
+            base = n * PASS * PACK - LAP * len([i for i in (2, 3, 5) if i <= n])
+            return woven[:, base:base + PASS * PACK]
 
         def weave(dst, src, width, vec_cols):
             for eng, lo, hi in ((0, 0, vec_cols), (1, vec_cols, width)):
@@ -93,20 +97,21 @@ def tile_list_tied_table_grad_pl_kernel(tc, h2, e, g_words, g_scales, w_words, w
                         nc.scalar.copy(out=o, in_=s)
 
         def weave_h(a):
-            hb = sb.tile([P, PACK, P, PACK], BF16, name="hb%d" % a, align_bytes=64)
-            o = hb[:].rearrange("p r m j -> p m j r")
-            s = h_raw[a][:].rearrange("p j (m r) -> p m j r", r=PACK)
-            v = H_VEC[a]
-            if v > 0:
-                nc.vector.tensor_copy(out=o[:, 0:v], in_=s[:, 0:v])
-            if v < P:
-                nc.scalar.copy(out=o[:, v:P], in_=s[:, v:P])
+            hb = slab(ORDER[("h", a)])
+            o = hb.rearrange("p (r m j) -> p m j r", r=PACK, j=PACK)
+            if a == 0:
+                for u in range(2):
+                    nc.scalar.copy(out=o[:, 64 * u:64 * u + 64], in_=h_first[u][:].rearrange("p j (m r) -> p m j r", r=PACK))
+            else:
+                s = h_raw1[:].rearrange("p j (m r) -> p m j r", r=PACK)
+                nc.vector.tensor_copy(out=o[:, 0:H_VEC], in_=s[:, 0:H_VEC])
+                nc.scalar.copy(out=o[:, H_VEC:P], in_=s[:, H_VEC:P])
             return hb
 
         def quant_h(a, hb):
             codes = sb.tile([P, K], U32, name="h_codes%d" % a, align_bytes=64)
             plane = sb.tile([P, K], U8, name="h_plane%d" % a, align_bytes=64)
-            nc.vector.quantize_mx(out=codes[:].bitcast(E4M3), scales=plane[:], in_=hb[:].rearrange("p r m j -> p (r m j)"))
+            nc.vector.quantize_mx(out=codes[:].bitcast(E4M3), scales=plane[:], in_=hb)
             return codes, plane
 
         def e_tiles(a, half):
@@ -114,8 +119,8 @@ def tile_list_tied_table_grad_pl_kernel(tc, h2, e, g_words, g_scales, w_words, w
             plane = sb.tile([P, HALF], U8, name="e_plane%d%d" % (a, half), align_bytes=64)
             return codes, plane
 
-        def weave_e(name, raw, width, vec_cols):
-            eb = sb.tile([P, width, PACK], BF16, name=name, align_bytes=64)
+        def weave_e(name, raw, width, vec_cols, tag):
+            eb = sb.tile([P, width, PACK], BF16, name=name, tag=tag, align_bytes=64)
             weave(eb, raw, width, vec_cols)
             return eb
 
@@ -133,48 +138,68 @@ def tile_list_tied_table_grad_pl_kernel(tc, h2, e, g_words, g_scales, w_words, w
         y_words = out_1[0].rearrange("p c r -> p (c r)").bitcast(I32)
         y_plane = sb.tile([P, V], U8, name="y_plane", align_bytes=64)
 
-        def finish(half, acc):
-            cols = slice(half * HALF, (half + 1) * HALF)
-            y = sb.tile([P, PACK, HALF], F32, name="y%d" % half)
-            for r in range(PACK):
-                nc.vector.scalar_tensor_tensor(out=y[:, r, :], in0=acc[r][:], scalar=ALPHA, in1=pages[r][:, cols], op0=MULT, op1=ADD)
-                nc.sync.dma_start(out=y_rows[:, r, cols], in_=y[:, r, :])
-            yb = sb.tile([P, HALF, PACK], BF16, name="yb%d" % half, align_bytes=64)
-            weave(yb, y, HALF, Y_VEC[half])
-            codes = sb.tile([P, HALF], U32, name="y_codes%d" % half, align_bytes=64)
-            nc.vector.quantize_mx(out=codes[:].bitcast(E4M3), scales=y_plane[:, cols], in_=yb[:].rearrange("p c j -> p (c j)"))
-            nc.sync.dma_start(out=y_words[:, cols], in_=codes[:].bitcast(I32))
+        def combine(half, acc, y, r, lo, hi):
+            nc.vector.scalar_tensor_tensor(out=y[:, r, lo:hi], in0=acc[r][:, lo:hi], scalar=ALPHA,
+                                           in1=pages[r][:, half * HALF + lo:half * HALF + hi], op0=MULT, op1=ADD)
+
+        def store_y(half, y, r):
+            nc.sync.dma_start(out=y_rows[:, r, half * HALF:(half + 1) * HALF], in_=y[:, r, :])
+
+        def quant_y(yb, c0, width, tag):
+            codes = sb.tile([P, width], U32, name="y_codes%d" % c0, tag=tag, align_bytes=64)
+            nc.vector.quantize_mx(out=codes[:].bitcast(E4M3), scales=y_plane[:, c0:c0 + width], in_=yb[:].rearrange("p c j -> p (c j)"))
+            nc.sync.dma_start(out=y_words[:, c0:c0 + width], in_=codes[:].bitcast(I32))
+
+        def operand_e(a, half):
+            if half == 0:
+                eb = slab(ORDER[(a, half)]).rearrange("p (c j) -> p c j", j=PACK)
+                weave(eb, e_raw[(a, half)], HALF, E_VEC[(a, half)])
+            else:
+                eb = weave_e("eb%d1" % a, e_raw[(a, half)], HALF, E_VEC[(a, half)], "late")
+            eq = e_tiles(a, half)
+            return eb, eq
 
         acc0 = [ps.tile([P, HALF], F32, name="acc0_%d" % r, tag="bank%d" % r) for r in range(PACK)]
-
-        eq00 = e_tiles(0, 0)
-        for u in range(2):
-            eb = weave_e("eb00_%d" % u, first_raw[u], 256, FIRST_VEC[u])
-            quant_e(eb, eq00, 256 * u, 256)
+        hb = weave_h(0)
         for r in range(PACK):
             nc.vector.tensor_copy(pages[r][:].indirect(offsets[:]), dx[:, r, :])
-        hb = weave_h(0)
         hq0 = quant_h(0, hb)
+        eb, eq00 = operand_e(0, 0)
+        quant_e(eb, eq00, 0, HALF)
         passes(acc0, 0, hq0, eq00)
         hb = weave_h(1)
         hq1 = quant_h(1, hb)
-        eb = weave_e("eb10", e_raw[(1, 0)], HALF, E_VEC[(1, 0)])
-        eq10 = e_tiles(1, 0)
+        eb, eq10 = operand_e(1, 0)
         quant_e(eb, eq10, 0, HALF)
         passes(acc0, 1, hq1, eq10)
 
         acc1 = [ps.tile([P, HALF], F32, name="acc1_%d" % r, tag="bank%d" % (4 + r)) for r in range(PACK)]
-        eb = weave_e("eb01", e_raw[(0, 1)], HALF, E_VEC[(0, 1)])
-        finish(0, acc0)
-        eq01 = e_tiles(0, 1)
-        quant_e(eb, eq01, 0, HALF)
+        eb01, eq01 = operand_e(0, 1)
+        y0 = sb.tile([P, PACK, HALF], F32, name="y0")
+        for r in range(PACK):
+            combine(0, acc0, y0, r, 0, HALF)
+            store_y(0, y0, r)
+        yb0 = weave_e("yb0", y0, HALF, 0, "yb0")
+        quant_e(eb01, eq01, 0, HALF)
         passes(acc1, 0, hq0, eq01)
-        eq11 = e_tiles(1, 1)
-        for u in range(2):
-            eb = weave_e("eb11_%d" % u, last_raw[u], 256, LAST_VEC[u])
-            quant_e(eb, eq11, 256 * u, 256)
+        eb11, eq11 = operand_e(1, 1)
+        quant_e(eb11, eq11, 0, HALF)
         passes(acc1, 1, hq1, eq11)
-        finish(1, acc1)
+        quant_y(yb0, 0, HALF, "late")
+
+        y1 = sb.tile([P, PACK, HALF], F32, name="y1")
+        for r in range(2):
+            combine(1, acc1, y1, r, 0, HALF)
+            store_y(1, y1, r)
+        for r in range(2, PACK):
+            combine(1, acc1, y1, r, 0, 256)
+        yb1a = weave_e("yb1a", y1[:, :, 0:256], 256, 0, "yb1a")
+        for r in range(2, PACK):
+            combine(1, acc1, y1, r, 256, HALF)
+            store_y(1, y1, r)
+        yb1b = weave_e("yb1b", y1[:, :, 256:HALF], 256, 256, "yb1b")
+        quant_y(yb1a, HALF, 256, "yc1a")
+        quant_y(yb1b, HALF + 256, 256, "yc1b")
         for q in range(4):
             eng = nc.sync if q % 2 == 0 else nc.scalar
             eng.dma_start(out=out_2[0, 4 * q:4 * q + 4, :].bitcast(I32), in_=y_plane[32 * q:32 * q + 4, :].bitcast(I32))

@@ -22,11 +22,6 @@ PACK = 4
 PASS = P * PACK
 HALF = 512
 ALPHA = 0.03
-LAP = 32
-ORDER = {("h", 0): 0, (0, 0): 1, ("h", 1): 2, (1, 0): 3, (0, 1): 4, (1, 1): 5}
-
-H_VEC = 64
-E_VEC = {(0, 0): 0, (1, 0): 320, (0, 1): 0, (1, 1): 512}
 
 
 def tile_list_tied_table_grad_pl_kernel(tc, h2, e, g_words, g_scales, w_words, w_scales, offs, out_0, out_1, out_2):
@@ -54,16 +49,13 @@ def tile_list_tied_table_grad_pl_kernel(tc, h2, e, g_words, g_scales, w_words, w
             load_plane(nc.scalar, ws_raw, w_scales, q)
         nc.sync.dma_start(out=w_raw[:], in_=w_words[0].rearrange("p c r -> p (c r)").bitcast(I32))
         nc.sync.dma_start(out=g_codes[:].bitcast(I32), in_=g_words[0].bitcast(I32))
-        load_plane(nc.sync, g_plane, g_scales, 0)
-        h_first = [load_rows("h_first0", h2, 0, 0, 256)]
-        for q in range(1, 4):
-            load_plane(nc.sync, g_plane, g_scales, q)
-        h_first.append(load_rows("h_first1", h2, 0, 256, 256))
         nc.sync.dma_start(offsets[:], offs)
-        e_raw = {(0, 0): load_rows("e_raw00", e, 0, 0, HALF)}
-        h_raw1 = load_rows("h_raw1", h2, 1, 0, K)
-        for a, half in ((1, 0), (0, 1), (1, 1)):
-            e_raw[(a, half)] = load_rows("e_raw%d%d" % (a, half), e, a, half * HALF, HALF)
+        e_raw00 = load_rows("e_raw00", e, 0, 0, HALF)
+        for q in range(4):
+            load_plane(nc.sync, g_plane, g_scales, q)
+        h_raw = [load_rows("h_raw%d" % a, h2, a, 0, K) for a in range(2)]
+        e_raw10 = [load_rows("e_raw10_%d" % u, e, 1, 256 * u, 256) for u in range(2)]
+        e_raw1 = [load_rows("e_raw%d1" % a, e, a, HALF, HALF) for a in range(2)]
 
         pages = [sb.tile([P, V], F32, name="page%d" % r) for r in range(PACK)]
         for r in range(PACK):
@@ -80,12 +72,6 @@ def tile_list_tied_table_grad_pl_kernel(tc, h2, e, g_words, g_scales, w_words, w
         dx = sb.tile([P, PACK, J], F32, name="dx")
         nc.vector.tensor_copy(out=dx[:], in_=dx_ps[:])
 
-        woven = sb.tile([P, 4 * PASS * PACK], BF16, name="woven", align_bytes=64)
-
-        def slab(n):
-            base = n * PASS * PACK - LAP * len([i for i in (2, 3, 5) if i <= n])
-            return woven[:, base:base + PASS * PACK]
-
         def weave(dst, src, width, vec_cols):
             for eng, lo, hi in ((0, 0, vec_cols), (1, vec_cols, width)):
                 if hi > lo:
@@ -97,21 +83,14 @@ def tile_list_tied_table_grad_pl_kernel(tc, h2, e, g_words, g_scales, w_words, w
                         nc.scalar.copy(out=o, in_=s)
 
         def weave_h(a):
-            hb = slab(ORDER[("h", a)])
-            o = hb.rearrange("p (r m j) -> p m j r", r=PACK, j=PACK)
-            if a == 0:
-                for u in range(2):
-                    nc.scalar.copy(out=o[:, 64 * u:64 * u + 64], in_=h_first[u][:].rearrange("p j (m r) -> p m j r", r=PACK))
-            else:
-                s = h_raw1[:].rearrange("p j (m r) -> p m j r", r=PACK)
-                nc.vector.tensor_copy(out=o[:, 0:H_VEC], in_=s[:, 0:H_VEC])
-                nc.scalar.copy(out=o[:, H_VEC:P], in_=s[:, H_VEC:P])
+            hb = sb.tile([P, PACK, P, PACK], BF16, name="hb%d" % a, tag="hb%d" % a, align_bytes=64)
+            nc.scalar.copy(out=hb[:].rearrange("p r m j -> p m j r"), in_=h_raw[a][:].rearrange("p j (m r) -> p m j r", r=PACK))
             return hb
 
         def quant_h(a, hb):
             codes = sb.tile([P, K], U32, name="h_codes%d" % a, align_bytes=64)
             plane = sb.tile([P, K], U8, name="h_plane%d" % a, align_bytes=64)
-            nc.vector.quantize_mx(out=codes[:].bitcast(E4M3), scales=plane[:], in_=hb)
+            nc.vector.quantize_mx(out=codes[:].bitcast(E4M3), scales=plane[:], in_=hb[:].rearrange("p r m j -> p (r m j)"))
             return codes, plane
 
         def e_tiles(a, half):
@@ -150,31 +129,24 @@ def tile_list_tied_table_grad_pl_kernel(tc, h2, e, g_words, g_scales, w_words, w
             nc.vector.quantize_mx(out=codes[:].bitcast(E4M3), scales=y_plane[:, c0:c0 + width], in_=yb[:].rearrange("p c j -> p (c j)"))
             nc.sync.dma_start(out=y_words[:, c0:c0 + width], in_=codes[:].bitcast(I32))
 
-        def operand_e(a, half):
-            if half == 0:
-                eb = slab(ORDER[(a, half)]).rearrange("p (c j) -> p c j", j=PACK)
-                weave(eb, e_raw[(a, half)], HALF, E_VEC[(a, half)])
-            else:
-                eb = weave_e("eb%d1" % a, e_raw[(a, half)], HALF, E_VEC[(a, half)], "late")
-            eq = e_tiles(a, half)
-            return eb, eq
-
         acc0 = [ps.tile([P, HALF], F32, name="acc0_%d" % r, tag="bank%d" % r) for r in range(PACK)]
-        hb = weave_h(0)
+        eb = weave_e("eb00", e_raw00, HALF, 256, "eb00")
         for r in range(PACK):
             nc.vector.tensor_copy(pages[r][:].indirect(offsets[:]), dx[:, r, :])
-        hq0 = quant_h(0, hb)
-        eb, eq00 = operand_e(0, 0)
+        eq00 = e_tiles(0, 0)
         quant_e(eb, eq00, 0, HALF)
+        hq0 = quant_h(0, weave_h(0))
         passes(acc0, 0, hq0, eq00)
-        hb = weave_h(1)
-        hq1 = quant_h(1, hb)
-        eb, eq10 = operand_e(1, 0)
-        quant_e(eb, eq10, 0, HALF)
+        hb1 = weave_h(1)
+        eb10 = [weave_e("eb10_0", e_raw10[0], 256, 256, "hb0"), weave_e("eb10_1", e_raw10[1], 256, 0, "eb10_1")]
+        hq1 = quant_h(1, hb1)
+        eq10 = e_tiles(1, 0)
+        for u in range(2):
+            quant_e(eb10[u], eq10, 256 * u, 256)
         passes(acc0, 1, hq1, eq10)
 
         acc1 = [ps.tile([P, HALF], F32, name="acc1_%d" % r, tag="bank%d" % (4 + r)) for r in range(PACK)]
-        eb01, eq01 = operand_e(0, 1)
+        eb01, eq01 = weave_e("eb01", e_raw1[0], HALF, 0, "late"), e_tiles(0, 1)
         y0 = sb.tile([P, PACK, HALF], F32, name="y0")
         for r in range(PACK):
             combine(0, acc0, y0, r, 0, HALF)
@@ -182,7 +154,7 @@ def tile_list_tied_table_grad_pl_kernel(tc, h2, e, g_words, g_scales, w_words, w
         yb0 = weave_e("yb0", y0, HALF, 0, "yb0")
         quant_e(eb01, eq01, 0, HALF)
         passes(acc1, 0, hq0, eq01)
-        eb11, eq11 = operand_e(1, 1)
+        eb11, eq11 = weave_e("eb11", e_raw1[1], HALF, HALF, "late"), e_tiles(1, 1)
         quant_e(eb11, eq11, 0, HALF)
         passes(acc1, 1, hq1, eq11)
         quant_y(yb0, 0, HALF, "late")

from contextlib import ExitStack

import concourse.mybir as mybir

T, K, V, N, J = 1024, 512, 1024, 512, 128
FLOPS = 2 * T * K * V + 2 * N * K * J

F32 = mybir.dt.float32
BF16 = mybir.dt.bfloat16
I32 = mybir.dt.int32
U32 = mybir.dt.uint32
U16 = mybir.dt.uint16
U8 = mybir.dt.uint8
E4M3 = mybir.dt.float8_e4m3fn_x4
E5M2 = mybir.dt.float8_e5m2_x4
E2M1 = mybir.dt.float4_e2m1fn_x4
MULT = mybir.AluOpType.mult
ADD = mybir.AluOpType.add

P = 128
PACK = 4
PASS = P * PACK
HALF = 512
ALPHA = 0.03


def tile_list_tied_table_grad_pl_kernel(tc, h2, e, g_words, g_scales, w_words, w_scales, offs, out_0, out_1, out_2):
    nc = tc.nc
    with ExitStack() as ctx:
        sb = ctx.enter_context(tc.tile_pool(name="sb", bufs=1))
        ps = ctx.enter_context(tc.psum_pool(name="ps", bufs=1))

        offsets = sb.tile([P, J // 16], U16, name="offsets")
        w_raw = sb.tile([P, K], I32, name="w_raw", align_bytes=64)
        g_codes = sb.tile([P, 2 * J], U8, name="g_codes", align_bytes=64)
        ws_raw = sb.tile([P, K], U8, name="ws_raw", align_bytes=64)
        g_plane = sb.tile([P, J], U8, name="g_plane", align_bytes=64)

        def load_plane(eng, tile, scales, q):
            rows = scales[0, 4 * q:4 * q + 4, :].bitcast(I32)
            eng.dma_start(out=tile[32 * q:32 * q + 32, :].bitcast(I32), in_=rows.unsqueeze(0).broadcast_to([8, 4, rows.shape[1]]))

        def load_rows(name, src, a, c0, width):
            raw = sb.tile([P, PACK, width], F32, name=name, tag=name, align_bytes=64)
            nc.sync.dma_start(out=raw[:], in_=src[a * PASS:(a + 1) * PASS, c0:c0 + width].rearrange("(p j) c -> p j c", j=PACK))
            return raw

        for q in range(4):
            load_plane(nc.scalar, ws_raw, w_scales, q)
        nc.sync.dma_start(out=w_raw[:], in_=w_words[0].rearrange("p c r -> p (c r)").bitcast(I32))
        nc.sync.dma_start(out=g_codes[:].bitcast(I32), in_=g_words[0].bitcast(I32))
        nc.sync.dma_start(offsets[:], offs)
        e_raw00 = load_rows("e_raw00", e, 0, 0, HALF)
        for q in range(4):
            load_plane(nc.sync, g_plane, g_scales, q)
        h_raw = [load_rows("h_raw%d" % a, h2, a, 0, K) for a in range(2)]
        e_raw10 = [load_rows("e_raw10_%d" % u, e, 1, 256 * u, 256) for u in range(2)]
        e_raw1 = [load_rows("e_raw%d1" % a, e, a, HALF, HALF) for a in range(2)]

        pages = [sb.tile([P, V], F32, name="page%d" % r) for r in range(PACK)]
        for r in range(PACK):
            (nc.vector if r < 2 else nc.gpsimd).memset(pages[r][:], 0.0)

        w_codes = sb.tile([P, PACK, P], I32, name="w_codes", align_bytes=64)
        w_plane = sb.tile([P, PACK, P], U8, name="w_plane", align_bytes=64)
        nc.vector.tensor_copy(out=w_codes[:].rearrange("p r m -> p m r"), in_=w_raw[:].rearrange("p (m r) -> p m r", r=PACK))
        nc.vector.tensor_copy(out=w_plane[:], in_=ws_raw[:].rearrange("p (m r) -> p r m", r=PACK))
        dx_ps = ps.tile([P, PACK, J], F32, name="dx_ps", tag="bank7")
        for r in range(PACK):
            nc.tensor.matmul_mx(out=dx_ps[:, r, :], lhsT=w_codes[:, r, :].bitcast(E4M3), lhsT_scale=w_plane[:, r, :],
                                rhs=g_codes[:].bitcast(E2M1), rhs_scale=g_plane[:], start=True, stop=True)
        dx = sb.tile([P, PACK, J], F32, name="dx")
        nc.vector.tensor_copy(out=dx[:], in_=dx_ps[:])

        def weave(dst, src, width, vec_cols):
            for eng, lo, hi in ((0, 0, vec_cols), (1, vec_cols, width)):
                if hi > lo:
                    o = dst[:, lo:hi, :].rearrange("p (c i) j -> p c j i", i=4)
                    s = src[:, :, lo:hi].rearrange("p j (c i) -> p c j i", i=4)
                    if eng == 0:
                        nc.vector.tensor_copy(out=o, in_=s)
                    else:
                        nc.scalar.copy(out=o, in_=s)

        def weave_h(a):
            hb = sb.tile([P, PACK, P, PACK], BF16, name="hb%d" % a, tag="hb%d" % a, align_bytes=64)
            nc.scalar.copy(out=hb[:].rearrange("p r m j -> p m j r"), in_=h_raw[a][:].rearrange("p j (m r) -> p m j r", r=PACK))
            return hb

        def quant_h(a, hb):
            codes = sb.tile([P, K], U32, name="h_codes%d" % a, align_bytes=64)
            plane = sb.tile([P, K], U8, name="h_plane%d" % a, align_bytes=64)
            nc.vector.quantize_mx(out=codes[:].bitcast(E4M3), scales=plane[:], in_=hb[:].rearrange("p r m j -> p (r m j)"))
            return codes, plane

        def e_tiles(a, half):
            codes = sb.tile([P, HALF], U32, name="e_codes%d%d" % (a, half), align_bytes=64)
            plane = sb.tile([P, HALF], U8, name="e_plane%d%d" % (a, half), align_bytes=64)
            return codes, plane

        def weave_e(name, raw, width, vec_cols, tag):
            eb = sb.tile([P, width, PACK], BF16, name=name, tag=tag, align_bytes=64)
            weave(eb, raw, width, vec_cols)
            return eb

        def quant_e(eb, tiles, c0, width):
            nc.vector.quantize_mx(out=tiles[0][:, c0:c0 + width].bitcast(E5M2), scales=tiles[1][:, c0:c0 + width],
                                  in_=eb[:].rearrange("p c j -> p (c j)"))

        def passes(acc, a, hq, eq):
            for r in range(PACK):
                cols = slice(r * P, (r + 1) * P)
                nc.tensor.matmul_mx(out=acc[r][:], lhsT=hq[0][:, cols].bitcast(E4M3), lhsT_scale=hq[1][:, cols],
                                    rhs=eq[0][:].bitcast(E5M2), rhs_scale=eq[1][:], start=(a == 0), stop=(a == 1))

        y_rows = out_0.rearrange("(p r) v -> p r v", r=PACK)
        y_words = out_1[0].rearrange("p c r -> p (c r)").bitcast(I32)
        y_plane = sb.tile([P, V], U8, name="y_plane", align_bytes=64)

        def combine(half, acc, y, r, lo, hi):
            nc.vector.scalar_tensor_tensor(out=y[:, r, lo:hi], in0=acc[r][:, lo:hi], scalar=ALPHA,
                                           in1=pages[r][:, half * HALF + lo:half * HALF + hi], op0=MULT, op1=ADD)

        def store_y(half, y, r):
            nc.sync.dma_start(out=y_rows[:, r, half * HALF:(half + 1) * HALF], in_=y[:, r, :])

        def quant_y(yb, c0, width, tag):
            codes = sb.tile([P, width], U32, name="y_codes%d" % c0, tag=tag, align_bytes=64)
            nc.vector.quantize_mx(out=codes[:].bitcast(E4M3), scales=y_plane[:, c0:c0 + width], in_=yb[:].rearrange("p c j -> p (c j)"))
            nc.sync.dma_start(out=y_words[:, c0:c0 + width], in_=codes[:].bitcast(I32))

        acc0 = [ps.tile([P, HALF], F32, name="acc0_%d" % r, tag="bank%d" % r) for r in range(PACK)]
        eb = weave_e("eb00", e_raw00, HALF, 256, "eb00")
        for r in range(PACK):
            nc.vector.tensor_copy(pages[r][:].indirect(offsets[:]), dx[:, r, :])
        eq00 = e_tiles(0, 0)
        quant_e(eb, eq00, 0, HALF)
        hq0 = quant_h(0, weave_h(0))
        passes(acc0, 0, hq0, eq00)
        hb1 = weave_h(1)
        eb10 = [weave_e("eb10_0", e_raw10[0], 256, 256, "hb0"), weave_e("eb10_1", e_raw10[1], 256, 0, "eb10_1")]
        hq1 = quant_h(1, hb1)
        eq10 = e_tiles(1, 0)
        for u in range(2):
            quant_e(eb10[u], eq10, 256 * u, 256)
        passes(acc0, 1, hq1, eq10)

        acc1 = [ps.tile([P, HALF], F32, name="acc1_%d" % r, tag="bank%d" % (4 + r)) for r in range(PACK)]
        eb01, eq01 = weave_e("eb01", e_raw1[0], HALF, 0, "late"), e_tiles(0, 1)
        y0 = sb.tile([P, PACK, HALF], F32, name="y0")
        for r in range(PACK):
            combine(0, acc0, y0, r, 0, HALF)
            store_y(0, y0, r)
        yb0 = weave_e("yb0", y0, HALF, 0, "yb0")
        quant_e(eb01, eq01, 0, HALF)
        passes(acc1, 0, hq0, eq01)
        eb11, eq11 = weave_e("eb11", e_raw1[1], HALF, HALF, "late"), e_tiles(1, 1)
        quant_e(eb11, eq11, 0, HALF)
        passes(acc1, 1, hq1, eq11)
        quant_y(yb0, 0, HALF, "late")

        y1 = sb.tile([P, PACK, HALF], F32, name="y1")
        for r in range(2):
            combine(1, acc1, y1, r, 0, HALF)
            store_y(1, y1, r)
        for r in range(2, PACK):
            combine(1, acc1, y1, r, 0, 256)
        yb1a = weave_e("yb1a", y1[:, :, 0:256], 256, 0, "yb1a")
        for r in range(2, PACK):
            combine(1, acc1, y1, r, 256, HALF)
            store_y(1, y1, r)
        yb1b = weave_e("yb1b", y1[:, :, 256:HALF], 256, 256, "yb1b")
        quant_y(yb1a, HALF, 256, "yc1a")
        quant_y(yb1b, HALF + 256, 256, "yc1b")
        for q in range(4):
            eng = nc.sync if q % 2 == 0 else nc.scalar
            eng.dma_start(out=out_2[0, 4 * q:4 * q + 4, :].bitcast(I32), in_=y_plane[32 * q:32 * q + 4, :].bitcast(I32))
